import numpy as np
import ml_dtypes


def mxq(x, axis, fmt="e4m3"):
    dtype, down = {"e4m3": (ml_dtypes.float8_e4m3fn, 7), "e5m2": (ml_dtypes.float8_e5m2, 14)}[fmt]
    v = np.moveaxis(np.asarray(x, np.float32).astype(ml_dtypes.bfloat16).astype(np.float64), axis, -1)
    blocks = v.reshape(v.shape[:-1] + (-1, 32))
    amax = np.abs(blocks).max(-1, keepdims=True)
    byte = np.maximum(np.where(amax > 0, np.frexp(amax)[1] - 1 + 127, 0) - down, 1)
    scale = np.exp2(byte - 127.0)
    codes = (blocks / scale).astype(np.float32).astype(dtype).astype(np.float64)
    return np.moveaxis((codes * scale).reshape(v.shape), -1, axis)


WIDE = False


def mx_kscale(k):
    if not WIDE:
        return np.ones(k)
    levels = np.array([10, -10, 5, -5, 0])
    if k % 512:
        return np.exp2(np.random.permutation(np.resize(levels, k // 32))).repeat(32)
    a = np.empty((k // 512, 16))
    for p in range(k // 512):
        a[p, :8] = np.random.permutation(np.resize(levels, 8))
        for g in range(8):
            far = levels[np.abs(levels - a[p, g]) >= 10]
            a[p, g + 8] = far[np.random.randint(len(far))]
    return np.exp2(a.ravel()).repeat(32)


def f64(x):
    return np.asarray(x).astype(np.float64)


def striped(idx):
    return np.tile(np.asarray(idx).reshape(-1, 16).T, (8, 1)).astype(np.uint16)


def unstriped(offs):
    return offs[:16].T.reshape(-1).astype(np.int64)


E2M1 = np.array([0.0, 0.5, 1.0, 1.5, 2.0, 3.0, 4.0, 6.0, -0.0, -0.5, -1.0, -1.5, -2.0, -3.0, -4.0, -6.0])


def pack_weight(w, fmt):
    k, n = w.shape
    w = f64(np.asarray(w, np.float32).astype(ml_dtypes.bfloat16)).reshape(k // 32, 32, n)
    amax = np.abs(w).max(1)
    if fmt == "e4m3":
        byte = np.frexp(amax)[1] - 1 + 127 - 7
    else:
        mant, ex = np.frexp(amax / 6.0)
        byte = np.where(mant > 0.5, ex, ex - 1) + 127
    byte = np.clip(np.where(amax > 0, byte, 1), 1, 254)
    scaled = (w * np.exp2(127.0 - byte)[:, None, :]).reshape(k, n).astype(np.float32)
    by_word = np.ascontiguousarray(scaled.reshape(k // 512, 128, 4, n).transpose(0, 1, 3, 2))
    if fmt == "e4m3":
        words = by_word.astype(ml_dtypes.float8_e4m3fn).view(np.uint8)
    else:
        c = by_word.astype(ml_dtypes.float4_e2m1fn).view(np.uint8) & 0xF
        words = (c[..., 0::2] | (c[..., 1::2] << 4)).reshape(k // 512, 128, 2 * n)
    return np.ascontiguousarray(words), np.ascontiguousarray(byte.astype(np.uint8).reshape(k // 512, 16, n))


def unpack_weight(words, scales, fmt):
    g, _, n = scales.shape
    words = np.ascontiguousarray(words).reshape(g, 128, n, -1)
    if fmt == "e4m3":
        vals = words.view(ml_dtypes.float8_e4m3fn).astype(np.float64)
    else:
        nib = np.empty((g, 128, n, 4), np.uint8)
        nib[..., 0::2] = words & 0xF
        nib[..., 1::2] = words >> 4
        vals = E2M1[nib]
    vals = vals * np.repeat(np.exp2(scales.astype(np.float64) - 127.0), 8, axis=1)[..., None]
    return vals.transpose(0, 1, 3, 2).reshape(g * 512, n)


D, E, T, I, Q = 512, 512, 2048, 512, 128


def setup_inputs():
    n = np.random.standard_normal
    idx = np.random.permutation(T)[:I]
    fd = mx_kscale(D)
    fe = mx_kscale(E)
    keysp = pack_weight(n((D, T)) / fd[:, None], "e2m1")
    valsp = pack_weight(n((E, T)) / fe[:, None], "e2m1")
    return {
        "query": (n((D, Q)) * 0.8 / np.sqrt(D) * fd[:, None]).astype(np.float32),
        "keys_words": keysp[0],
        "keys_scales": keysp[1],
        "bonus": (np.random.uniform(0.5, 2.0, (Q, 1))).astype(np.float32),
        "gout": (n((E, Q)) * 1 / np.sqrt(E) * fe[:, None]).astype(np.float32),
        "vals_words": valsp[0],
        "vals_scales": valsp[1],
        "old": (0.5 * n((Q, T))).astype(np.float32),
        "offs": striped(idx),
    }


def reference(query, keys_words, keys_scales, bonus, gout, vals_words, vals_scales, old, offs):
    idx = unstriped(offs)
    keysu = unpack_weight(keys_words, keys_scales, "e2m1")
    valsu = unpack_weight(vals_words, vals_scales, "e2m1")
    queryq = mxq(f64(query), 0, "e4m3")
    keysidxg = keysu[:, idx]
    a = queryq.T @ keysidxg
    b = a - np.max(a, axis=1, keepdims=True)
    p = np.exp(b)
    z = np.sum(p, axis=1, keepdims=True)
    goutq = mxq(f64(gout), 0, "e4m3")
    valsidxg = valsu[:, idx]
    c0 = goutq.T @ valsidxg
    dz = f64(bonus) / z - np.sum(p * c0, axis=1, keepdims=True) / np.square(z) - f64(bonus) * (-1.0) * np.sum(p * b, axis=1, keepdims=True) / np.square(z)
    dp = 1.0 / z * c0 + f64(bonus) * (-1.0) / z * b + dz
    db = f64(bonus) * (-1.0) / z * p + dp * p
    gs = db * 512.0
    gf = np.zeros((Q, T))
    gf[:, idx] = gs
    y = f64(old) + gf
    return y

@@ -1,0 +1,129 @@
+from contextlib import ExitStack
+
+import concourse.mybir as mybir
+
+D, E, T, I, Q = 512, 512, 2048, 512, 128
+FLOPS = 2 * Q * I * (D + E)
+
+F32 = mybir.dt.float32
+BF16 = mybir.dt.bfloat16
+I32 = mybir.dt.int32
+U32 = mybir.dt.uint32
+U16 = mybir.dt.uint16
+U8 = mybir.dt.uint8
+FP8X4 = mybir.dt.float8_e4m3fn_x4
+FP4X4 = mybir.dt.float4_e2m1fn_x4
+ALU = mybir.AluOpType
+ACT = mybir.ActivationFunctionType
+
+P = 128
+PACK = 4
+HALF = I // 2
+STORE_WIDTHS = (256, 512, 512, 512, 256)
+
+
+def tile_attend_bentropybonus_s_kernel(tc, query, keys_words, keys_scales, bonus, gout, vals_words, vals_scales, old, offs, out):
+    nc = tc.nc
+
+    with ExitStack() as ctx:
+        sb = ctx.enter_context(tc.tile_pool(name="sb", bufs=1))
+        psum = ctx.enter_context(tc.psum_pool(name="psum", bufs=1))
+
+        def load_scales(queue, plane, scales):
+            for quad in range(4):
+                queue.dma_start(out=plane[32 * quad : 32 * quad + 4, :].bitcast(I32), in_=scales[0, 4 * quad : 4 * quad + 4, :].bitcast(I32))
+
+        def interleave(grouped, raw):
+            nc.scalar.activation(grouped[:], raw[:].rearrange("p j w -> p w j"), ACT.Copy)
+
+        def quantize(codes, scales, grouped):
+            nc.vector.quantize_mx(out=codes[:].bitcast(FP8X4), scales=scales[:], in_=grouped[:].rearrange("p w j -> p (w j)"))
+
+        offsets = sb.tile([P, I // 16], U16, name="offsets")
+        nc.sync.dma_start(offsets[:], offs)
+
+        key_scale_pool = sb.tile([P, T], U8, name="key_scale_pool", align_bytes=64)
+        nc.vector.memset(key_scale_pool[:].bitcast(I32), 0)
+        val_scale_pool = sb.tile([P, T], U8, name="val_scale_pool", align_bytes=64)
+        nc.vector.memset(val_scale_pool[:].bitcast(I32), 0)
+        placed = sb.tile([P, T], F32, name="placed")
+        nc.vector.memset(placed[:], 0.0)
+
+        load_scales(nc.scalar, key_scale_pool, keys_scales)
+        query_raw = sb.tile([P, PACK, Q], F32, name="query_raw", tag="stage")
+        nc.sync.dma_start(out=query_raw[:], in_=query.rearrange("(p j) w -> p j w", j=PACK))
+        key_pool = sb.tile([P, T], U16, name="key_pool", tag="key_pool", align_bytes=64)
+        nc.sync.dma_start(out=key_pool[:].bitcast(I32), in_=keys_words[0].bitcast(I32))
+        val_pool = sb.tile([P, T], U16, name="val_pool", tag="val_pool", align_bytes=64)
+        nc.sync.dma_start(out=val_pool[:].bitcast(I32), in_=vals_words[0].bitcast(I32))
+        load_scales(nc.sync, val_scale_pool, vals_scales)
+
+        key_scales = sb.tile([P, I], U8, name="key_scales", align_bytes=64)
+        nc.vector.tensor_copy(key_scales[:], key_scale_pool[:].indirect(offsets[:]))
+
+        query_bf = sb.tile([P, Q, PACK], BF16, name="query_bf", tag="query_bf", align_bytes=64)
+        interleave(query_bf, query_raw)
+        gout_raw = sb.tile([P, PACK, Q], F32, name="gout_raw", tag="stage")
+        nc.scalar.dma_start(out=gout_raw[:], in_=gout.rearrange("(p j) w -> p j w", j=PACK))
+        query_codes = sb.tile([P, Q], U32, name="query_codes", align_bytes=64)
+        query_scales = sb.tile([P, Q], U8, name="query_scales", align_bytes=64)
+        quantize(query_codes, query_scales, query_bf)
+        bonus_col = sb.tile([P, 1], F32, name="bonus_col", tag="query_bf", align_bytes=64)
+        nc.sync.dma_start(out=bonus_col[:], in_=bonus)
+
+        key_words = sb.tile([P, I], U16, name="key_words", align_bytes=64)
+        nc.vector.tensor_copy(key_words[:], key_pool[:].indirect(offsets[:]))
+        scores = psum.tile([P, I], F32, name="scores")
+        nc.tensor.matmul_mx(out=scores[:], lhsT=query_codes[:].bitcast(FP8X4), lhsT_scale=query_scales[:],
+                            rhs=key_words[:].bitcast(FP4X4), rhs_scale=key_scales[:], start=True, stop=True)
+
+        val_words = sb.tile([P, I], U16, name="val_words", align_bytes=64)
+        nc.vector.tensor_copy(val_words[:], val_pool[:].indirect(offsets[:]))
+
+        gout_bf = sb.tile([P, Q, PACK], BF16, name="gout_bf", tag="gout_bf", align_bytes=64)
+        interleave(gout_bf, gout_raw)
+        neg_scores = sb.tile([P, I], F32, name="neg_scores", tag="val_pool", align_bytes=64)
+        neg_max = sb.tile([P, 1], F32, name="neg_max")
+        nc.vector.tensor_scalar(neg_scores[:], scores[:], -1.0, None, ALU.mult, ALU.min, accum_out=neg_max[:])
+        p = sb.tile([P, I], F32, name="p", tag="stage")
+        z = sb.tile([P, 1], F32, name="z")
+        nc.scalar.activation(p[:], neg_scores[:], ACT.Exp, bias=neg_max[:], scale=-1.0, accum_out=z[:])
+
+        old_sb = sb.tile([P, T], F32, name="old_sb", tag="key_pool", align_bytes=64)
+        nc.sync.dma_start(out=old_sb[:], in_=old)
+        gout_codes = sb.tile([P, Q], U32, name="gout_codes", align_bytes=64)
+        gout_scales = sb.tile([P, Q], U8, name="gout_scales", align_bytes=64)
+        quantize(gout_codes, gout_scales, gout_bf)
+
+        val_scales = sb.tile([P, I], U8, name="val_scales", tag="gout_bf", align_bytes=64)
+        u = sb.tile([P, I], F32, name="u")
+        halves = []
+        for h in range(2):
+            cols = slice(h * HALF, (h + 1) * HALF)
+            nc.vector.tensor_copy(val_scales[:, cols], val_scale_pool[:].indirect(offsets[:, h * HALF // 16 : (h + 1) * HALF // 16]))
+            c0 = psum.tile([P, HALF], F32, name="c0_%d" % h)
+            nc.tensor.matmul_mx(out=c0[:], lhsT=gout_codes[:].bitcast(FP8X4), lhsT_scale=gout_scales[:],
+                                rhs=val_words[:, cols].bitcast(FP4X4), rhs_scale=val_scales[:, cols], start=True, stop=True)
+            halves.append((cols, c0))
+        for cols, c0 in halves:
+            nc.vector.scalar_tensor_tensor(u[:, cols], neg_scores[:, cols], bonus_col[:], c0[:], ALU.mult, ALU.add)
+
+        pu = sb.tile([P, I], F32, name="pu")
+        s = sb.tile([P, 1], F32, name="s")
+        nc.vector.scalar_tensor_tensor(pu[:], p[:], 1.0, u[:], ALU.mult, ALU.mult, accum_out=s[:])
+        inv_z = sb.tile([P, 1], F32, name="inv_z")
+        nc.vector.reciprocal(inv_z[:], z[:])
+        w = sb.tile([P, I], F32, name="w")
+        nc.vector.tensor_scalar(w[:], u[:], z[:], s[:], ALU.mult, ALU.subtract)
+        row_factor = sb.tile([P, 1], F32, name="row_factor")
+        nc.vector.scalar_tensor_tensor(row_factor[:], inv_z[:], 512.0, inv_z[:], ALU.mult, ALU.mult)
+        nc.vector.tensor_tensor(placed[:].indirect(offsets[:]), p[:], w[:], ALU.mult)
+
+        first = 0
+        for n, width in enumerate(STORE_WIDTHS):
+            cols = slice(first, first + width)
+            result = sb.tile([P, width], F32, name="result_%d" % n)
+            nc.vector.scalar_tensor_tensor(result[:], placed[:, cols], row_factor[:], old_sb[:, cols], ALU.mult, ALU.add)
+            queue = nc.sync if n % 2 == 0 else nc.scalar
+            queue.dma_start(out=out[:, cols], in_=result[:])
+            first = first + width

@@ -18,7 +18,8 @@ ACT = mybir.ActivationFunctionType
 
 P = 128
 PACK = 4
-HALF = I // 2
+BLOCKS = 16
+FIRST_ROW = P - BLOCKS
 STORE_WIDTHS = (256, 512, 512, 512, 256)
 
 
@@ -29,9 +30,18 @@ def tile_attend_bentropybonus_s_kernel(tc, query, keys_words, keys_scales, bonus
         sb = ctx.enter_context(tc.tile_pool(name="sb", bufs=1))
         psum = ctx.enter_context(tc.psum_pool(name="psum", bufs=1))
 
-        def load_scales(queue, plane, scales):
+        def load_scale_pool(name, scales):
+            pool = sb.tile([P, T], U8, name=name, align_bytes=64)
+            nc.sync.dma_start(out=pool[FIRST_ROW:P, :].bitcast(I32), in_=scales[0].bitcast(I32))
+            nc.vector.memset(pool[0:FIRST_ROW, :].bitcast(I32), 0)
+            return pool
+
+        def gather_scales(name, pool, plane):
+            listed = sb.tile([P, I], U8, name=name, align_bytes=64)
+            nc.vector.tensor_copy(listed[:], pool[:].indirect(offsets[:]))
             for quad in range(4):
-                queue.dma_start(out=plane[32 * quad : 32 * quad + 4, :].bitcast(I32), in_=scales[0, 4 * quad : 4 * quad + 4, :].bitcast(I32))
+                first = FIRST_ROW + 4 * quad
+                nc.sync.dma_start(out=plane[32 * quad : 32 * quad + 4, :].bitcast(I32), in_=listed[first : first + 4, :].bitcast(I32))
 
         def interleave(grouped, raw):
             nc.scalar.activation(grouped[:], raw[:].rearrange("p j w -> p w j"), ACT.Copy)
@@ -41,35 +51,34 @@ def tile_attend_bentropybonus_s_kernel(tc, query, keys_words, keys_scales, bonus
 
         offsets = sb.tile([P, I // 16], U16, name="offsets")
         nc.sync.dma_start(offsets[:], offs)
+        key_scale_pool = load_scale_pool("key_scale_pool", keys_scales)
+        val_scale_pool = load_scale_pool("val_scale_pool", vals_scales)
+        bonus_col = sb.tile([P, 1], F32, name="bonus_col")
+        nc.scalar.dma_start(out=bonus_col[:], in_=bonus)
+        query_raw = sb.tile([P, PACK, Q], F32, name="query_raw")
+        nc.sync.dma_start(out=query_raw[:], in_=query.rearrange("(p j) w -> p j w", j=PACK))
+        key_pool = sb.tile([P, T], U16, name="key_pool", align_bytes=64)
+        nc.sync.dma_start(out=key_pool[:].bitcast(I32), in_=keys_words[0].bitcast(I32))
+        gout_raw = sb.tile([P, PACK, Q], F32, name="gout_raw", tag="gout_raw")
+        nc.sync.dma_start(out=gout_raw[:], in_=gout.rearrange("(p j) w -> p j w", j=PACK))
+        val_pool = sb.tile([P, T], U16, name="val_pool", tag="val_pool", align_bytes=64)
+        nc.sync.dma_start(out=val_pool[:].bitcast(I32), in_=vals_words[0].bitcast(I32))
 
-        key_scale_pool = sb.tile([P, T], U8, name="key_scale_pool", align_bytes=64)
-        nc.vector.memset(key_scale_pool[:].bitcast(I32), 0)
-        val_scale_pool = sb.tile([P, T], U8, name="val_scale_pool", align_bytes=64)
-        nc.vector.memset(val_scale_pool[:].bitcast(I32), 0)
+        key_scales = sb.tile([P, I], U8, name="key_scales", align_bytes=64)
+        nc.vector.memset(key_scales[:].bitcast(I32), 0)
+        val_scales = sb.tile([P, I], U8, name="val_scales", align_bytes=64)
+        nc.vector.memset(val_scales[:].bitcast(I32), 0)
         placed = sb.tile([P, T], F32, name="placed")
         nc.vector.memset(placed[:], 0.0)
 
-        load_scales(nc.scalar, key_scale_pool, keys_scales)
-        query_raw = sb.tile([P, PACK, Q], F32, name="query_raw", tag="stage")
-        nc.sync.dma_start(out=query_raw[:], in_=query.rearrange("(p j) w -> p j w", j=PACK))
-        key_pool = sb.tile([P, T], U16, name="key_pool", tag="key_pool", align_bytes=64)
-        nc.sync.dma_start(out=key_pool[:].bitcast(I32), in_=keys_words[0].bitcast(I32))
-        val_pool = sb.tile([P, T], U16, name="val_pool", tag="val_pool", align_bytes=64)
-        nc.sync.dma_start(out=val_pool[:].bitcast(I32), in_=vals_words[0].bitcast(I32))
-        load_scales(nc.sync, val_scale_pool, vals_scales)
+        gather_scales("key_scales_listed", key_scale_pool, key_scales)
+        gather_scales("val_scales_listed", val_scale_pool, val_scales)
 
-        key_scales = sb.tile([P, I], U8, name="key_scales", align_bytes=64)
-        nc.vector.tensor_copy(key_scales[:], key_scale_pool[:].indirect(offsets[:]))
-
-        query_bf = sb.tile([P, Q, PACK], BF16, name="query_bf", tag="query_bf", align_bytes=64)
+        query_bf = sb.tile([P, Q, PACK], BF16, name="query_bf", align_bytes=64)
         interleave(query_bf, query_raw)
-        gout_raw = sb.tile([P, PACK, Q], F32, name="gout_raw", tag="stage")
-        nc.scalar.dma_start(out=gout_raw[:], in_=gout.rearrange("(p j) w -> p j w", j=PACK))
         query_codes = sb.tile([P, Q], U32, name="query_codes", align_bytes=64)
         query_scales = sb.tile([P, Q], U8, name="query_scales", align_bytes=64)
         quantize(query_codes, query_scales, query_bf)
-        bonus_col = sb.tile([P, 1], F32, name="bonus_col", tag="query_bf", align_bytes=64)
-        nc.sync.dma_start(out=bonus_col[:], in_=bonus)
 
         key_words = sb.tile([P, I], U16, name="key_words", align_bytes=64)
         nc.vector.tensor_copy(key_words[:], key_pool[:].indirect(offsets[:]))
@@ -77,37 +86,29 @@ def tile_attend_bentropybonus_s_kernel(tc, query, keys_words, keys_scales, bonus
         nc.tensor.matmul_mx(out=scores[:], lhsT=query_codes[:].bitcast(FP8X4), lhsT_scale=query_scales[:],
                             rhs=key_words[:].bitcast(FP4X4), rhs_scale=key_scales[:], start=True, stop=True)
 
-        val_words = sb.tile([P, I], U16, name="val_words", align_bytes=64)
-        nc.vector.tensor_copy(val_words[:], val_pool[:].indirect(offsets[:]))
-
-        gout_bf = sb.tile([P, Q, PACK], BF16, name="gout_bf", tag="gout_bf", align_bytes=64)
+        gout_bf = sb.tile([P, Q, PACK], BF16, name="gout_bf", align_bytes=64)
         interleave(gout_bf, gout_raw)
-        neg_scores = sb.tile([P, I], F32, name="neg_scores", tag="val_pool", align_bytes=64)
-        neg_max = sb.tile([P, 1], F32, name="neg_max")
-        nc.vector.tensor_scalar(neg_scores[:], scores[:], -1.0, None, ALU.mult, ALU.min, accum_out=neg_max[:])
-        p = sb.tile([P, I], F32, name="p", tag="stage")
-        z = sb.tile([P, 1], F32, name="z")
-        nc.scalar.activation(p[:], neg_scores[:], ACT.Exp, bias=neg_max[:], scale=-1.0, accum_out=z[:])
-
-        old_sb = sb.tile([P, T], F32, name="old_sb", tag="key_pool", align_bytes=64)
-        nc.sync.dma_start(out=old_sb[:], in_=old)
         gout_codes = sb.tile([P, Q], U32, name="gout_codes", align_bytes=64)
         gout_scales = sb.tile([P, Q], U8, name="gout_scales", align_bytes=64)
         quantize(gout_codes, gout_scales, gout_bf)
 
-        val_scales = sb.tile([P, I], U8, name="val_scales", tag="gout_bf", align_bytes=64)
-        u = sb.tile([P, I], F32, name="u")
-        halves = []
-        for h in range(2):
-            cols = slice(h * HALF, (h + 1) * HALF)
-            nc.vector.tensor_copy(val_scales[:, cols], val_scale_pool[:].indirect(offsets[:, h * HALF // 16 : (h + 1) * HALF // 16]))
-            c0 = psum.tile([P, HALF], F32, name="c0_%d" % h)
-            nc.tensor.matmul_mx(out=c0[:], lhsT=gout_codes[:].bitcast(FP8X4), lhsT_scale=gout_scales[:],
-                                rhs=val_words[:, cols].bitcast(FP4X4), rhs_scale=val_scales[:, cols], start=True, stop=True)
-            halves.append((cols, c0))
-        for cols, c0 in halves:
-            nc.vector.scalar_tensor_tensor(u[:, cols], neg_scores[:, cols], bonus_col[:], c0[:], ALU.mult, ALU.add)
+        val_words = sb.tile([P, I], U16, name="val_words", tag="val_words", align_bytes=64)
+        nc.vector.tensor_copy(val_words[:], val_pool[:].indirect(offsets[:]))
+        c0 = psum.tile([P, I], F32, name="c0")
+        nc.tensor.matmul_mx(out=c0[:], lhsT=gout_codes[:].bitcast(FP8X4), lhsT_scale=gout_scales[:],
+                            rhs=val_words[:].bitcast(FP4X4), rhs_scale=val_scales[:], start=True, stop=True)
+        old_sb = sb.tile([P, T], F32, name="old_sb", tag="val_words", align_bytes=64)
+        nc.sync.dma_start(out=old_sb[:], in_=old)
 
+        neg_scores = sb.tile([P, I], F32, name="neg_scores", tag="val_pool", align_bytes=64)
+        neg_max = sb.tile([P, 1], F32, name="neg_max")
+        nc.vector.tensor_scalar(neg_scores[:], scores[:], -1.0, None, ALU.mult, ALU.min, accum_out=neg_max[:])
+        p = sb.tile([P, I], F32, name="p", tag="gout_raw")
+        z = sb.tile([P, 1], F32, name="z")
+        nc.scalar.activation(p[:], neg_scores[:], ACT.Exp, bias=neg_max[:], scale=-1.0, accum_out=z[:])
+
+        u = sb.tile([P, I], F32, name="u")
+        nc.vector.scalar_tensor_tensor(u[:], neg_scores[:], bonus_col[:], c0[:], ALU.mult, ALU.add)
         pu = sb.tile([P, I], F32, name="pu")
         s = sb.tile([P, 1], F32, name="s")
         nc.vector.scalar_tensor_tensor(pu[:], p[:], 1.0, u[:], ALU.mult, ALU.mult, accum_out=s[:])

@@ -20,7 +20,7 @@ P = 128
 PACK = 4
 BLOCKS = 16
 FIRST_ROW = P - BLOCKS
-STORE_WIDTHS = (256, 512, 512, 512, 256)
+STORE_WIDTHS = (256,) * 8
 
 
 def tile_attend_bentropybonus_s_kernel(tc, query, keys_words, keys_scales, bonus, gout, vals_words, vals_scales, old, offs, out):
@@ -53,11 +53,11 @@ def tile_attend_bentropybonus_s_kernel(tc, query, keys_words, keys_scales, bonus
         nc.sync.dma_start(offsets[:], offs)
         key_scale_pool = load_scale_pool("key_scale_pool", keys_scales)
         val_scale_pool = load_scale_pool("val_scale_pool", vals_scales)
-        bonus_col = sb.tile([P, 1], F32, name="bonus_col")
+        bonus_col = sb.tile([P, 1], F32, name="bonus_col", tag="bonus_col")
         nc.scalar.dma_start(out=bonus_col[:], in_=bonus)
         query_raw = sb.tile([P, PACK, Q], F32, name="query_raw")
         nc.sync.dma_start(out=query_raw[:], in_=query.rearrange("(p j) w -> p j w", j=PACK))
-        key_pool = sb.tile([P, T], U16, name="key_pool", align_bytes=64)
+        key_pool = sb.tile([P, T], U16, name="key_pool", tag="key_pool", align_bytes=64)
         nc.sync.dma_start(out=key_pool[:].bitcast(I32), in_=keys_words[0].bitcast(I32))
         gout_raw = sb.tile([P, PACK, Q], F32, name="gout_raw", tag="gout_raw")
         nc.sync.dma_start(out=gout_raw[:], in_=gout.rearrange("(p j) w -> p j w", j=PACK))
@@ -65,9 +65,7 @@ def tile_attend_bentropybonus_s_kernel(tc, query, keys_words, keys_scales, bonus
         nc.sync.dma_start(out=val_pool[:].bitcast(I32), in_=vals_words[0].bitcast(I32))
 
         key_scales = sb.tile([P, I], U8, name="key_scales", align_bytes=64)
-        nc.vector.memset(key_scales[:].bitcast(I32), 0)
         val_scales = sb.tile([P, I], U8, name="val_scales", align_bytes=64)
-        nc.vector.memset(val_scales[:].bitcast(I32), 0)
         placed = sb.tile([P, T], F32, name="placed")
         nc.vector.memset(placed[:], 0.0)
 
@@ -92,12 +90,12 @@ def tile_attend_bentropybonus_s_kernel(tc, query, keys_words, keys_scales, bonus
         gout_scales = sb.tile([P, Q], U8, name="gout_scales", align_bytes=64)
         quantize(gout_codes, gout_scales, gout_bf)
 
-        val_words = sb.tile([P, I], U16, name="val_words", tag="val_words", align_bytes=64)
+        val_words = sb.tile([P, I], U16, name="val_words", align_bytes=64)
         nc.vector.tensor_copy(val_words[:], val_pool[:].indirect(offsets[:]))
         c0 = psum.tile([P, I], F32, name="c0")
         nc.tensor.matmul_mx(out=c0[:], lhsT=gout_codes[:].bitcast(FP8X4), lhsT_scale=gout_scales[:],
                             rhs=val_words[:].bitcast(FP4X4), rhs_scale=val_scales[:], start=True, stop=True)
-        old_sb = sb.tile([P, T], F32, name="old_sb", tag="val_words", align_bytes=64)
+        old_sb = sb.tile([P, T], F32, name="old_sb", tag="key_pool", align_bytes=64)
         nc.sync.dma_start(out=old_sb[:], in_=old)
 
         neg_scores = sb.tile([P, I], F32, name="neg_scores", tag="val_pool", align_bytes=64)
@@ -112,7 +110,7 @@ def tile_attend_bentropybonus_s_kernel(tc, query, keys_words, keys_scales, bonus
         pu = sb.tile([P, I], F32, name="pu")
         s = sb.tile([P, 1], F32, name="s")
         nc.vector.scalar_tensor_tensor(pu[:], p[:], 1.0, u[:], ALU.mult, ALU.mult, accum_out=s[:])
-        inv_z = sb.tile([P, 1], F32, name="inv_z")
+        inv_z = sb.tile([P, 1], F32, name="inv_z", tag="bonus_col")
         nc.vector.reciprocal(inv_z[:], z[:])
         w = sb.tile([P, I], F32, name="w")
         nc.vector.tensor_scalar(w[:], u[:], z[:], s[:], ALU.mult, ALU.subtract)

from contextlib import ExitStack

import concourse.mybir as mybir

D, E, T, I, Q = 512, 512, 2048, 512, 128
FLOPS = 2 * Q * I * (D + E)

F32 = mybir.dt.float32
BF16 = mybir.dt.bfloat16
I32 = mybir.dt.int32
U32 = mybir.dt.uint32
U16 = mybir.dt.uint16
U8 = mybir.dt.uint8
FP8X4 = mybir.dt.float8_e4m3fn_x4
FP4X4 = mybir.dt.float4_e2m1fn_x4
ALU = mybir.AluOpType
ACT = mybir.ActivationFunctionType

P = 128
PACK = 4
BLOCKS = 16
FIRST_ROW = P - BLOCKS
STORE_WIDTHS = (256,) * 8


def tile_attend_bentropybonus_s_kernel(tc, query, keys_words, keys_scales, bonus, gout, vals_words, vals_scales, old, offs, out):
    nc = tc.nc

    with ExitStack() as ctx:
        sb = ctx.enter_context(tc.tile_pool(name="sb", bufs=1))
        psum = ctx.enter_context(tc.psum_pool(name="psum", bufs=1))

        def load_scale_pool(name, scales):
            pool = sb.tile([P, T], U8, name=name, align_bytes=64)
            nc.sync.dma_start(out=pool[FIRST_ROW:P, :].bitcast(I32), in_=scales[0].bitcast(I32))
            nc.vector.memset(pool[0:FIRST_ROW, :].bitcast(I32), 0)
            return pool

        def gather_scales(name, pool, plane):
            listed = sb.tile([P, I], U8, name=name, align_bytes=64)
            nc.vector.tensor_copy(listed[:], pool[:].indirect(offsets[:]))
            for quad in range(4):
                first = FIRST_ROW + 4 * quad
                nc.sync.dma_start(out=plane[32 * quad : 32 * quad + 4, :].bitcast(I32), in_=listed[first : first + 4, :].bitcast(I32))

        def interleave(grouped, raw):
            nc.scalar.activation(grouped[:], raw[:].rearrange("p j w -> p w j"), ACT.Copy)

        def quantize(codes, scales, grouped):
            nc.vector.quantize_mx(out=codes[:].bitcast(FP8X4), scales=scales[:], in_=grouped[:].rearrange("p w j -> p (w j)"))

        offsets = sb.tile([P, I // 16], U16, name="offsets")
        nc.sync.dma_start(offsets[:], offs)
        key_scale_pool = load_scale_pool("key_scale_pool", keys_scales)
        val_scale_pool = load_scale_pool("val_scale_pool", vals_scales)
        bonus_col = sb.tile([P, 1], F32, name="bonus_col", tag="bonus_col")
        nc.scalar.dma_start(out=bonus_col[:], in_=bonus)
        query_raw = sb.tile([P, PACK, Q], F32, name="query_raw")
        nc.sync.dma_start(out=query_raw[:], in_=query.rearrange("(p j) w -> p j w", j=PACK))
        key_pool = sb.tile([P, T], U16, name="key_pool", tag="key_pool", align_bytes=64)
        nc.sync.dma_start(out=key_pool[:].bitcast(I32), in_=keys_words[0].bitcast(I32))
        gout_raw = sb.tile([P, PACK, Q], F32, name="gout_raw", tag="gout_raw")
        nc.sync.dma_start(out=gout_raw[:], in_=gout.rearrange("(p j) w -> p j w", j=PACK))
        val_pool = sb.tile([P, T], U16, name="val_pool", tag="val_pool", align_bytes=64)
        nc.sync.dma_start(out=val_pool[:].bitcast(I32), in_=vals_words[0].bitcast(I32))

        key_scales = sb.tile([P, I], U8, name="key_scales", align_bytes=64)
        val_scales = sb.tile([P, I], U8, name="val_scales", align_bytes=64)
        placed = sb.tile([P, T], F32, name="placed")
        nc.vector.memset(placed[:], 0.0)

        gather_scales("key_scales_listed", key_scale_pool, key_scales)
        gather_scales("val_scales_listed", val_scale_pool, val_scales)

        query_bf = sb.tile([P, Q, PACK], BF16, name="query_bf", align_bytes=64)
        interleave(query_bf, query_raw)
        query_codes = sb.tile([P, Q], U32, name="query_codes", align_bytes=64)
        query_scales = sb.tile([P, Q], U8, name="query_scales", align_bytes=64)
        quantize(query_codes, query_scales, query_bf)

        key_words = sb.tile([P, I], U16, name="key_words", align_bytes=64)
        nc.vector.tensor_copy(key_words[:], key_pool[:].indirect(offsets[:]))
        scores = psum.tile([P, I], F32, name="scores")
        nc.tensor.matmul_mx(out=scores[:], lhsT=query_codes[:].bitcast(FP8X4), lhsT_scale=query_scales[:],
                            rhs=key_words[:].bitcast(FP4X4), rhs_scale=key_scales[:], start=True, stop=True)

        gout_bf = sb.tile([P, Q, PACK], BF16, name="gout_bf", align_bytes=64)
        interleave(gout_bf, gout_raw)
        gout_codes = sb.tile([P, Q], U32, name="gout_codes", align_bytes=64)
        gout_scales = sb.tile([P, Q], U8, name="gout_scales", align_bytes=64)
        quantize(gout_codes, gout_scales, gout_bf)

        val_words = sb.tile([P, I], U16, name="val_words", align_bytes=64)
        nc.vector.tensor_copy(val_words[:], val_pool[:].indirect(offsets[:]))
        c0 = psum.tile([P, I], F32, name="c0")
        nc.tensor.matmul_mx(out=c0[:], lhsT=gout_codes[:].bitcast(FP8X4), lhsT_scale=gout_scales[:],
                            rhs=val_words[:].bitcast(FP4X4), rhs_scale=val_scales[:], start=True, stop=True)
        old_sb = sb.tile([P, T], F32, name="old_sb", tag="key_pool", align_bytes=64)
        nc.sync.dma_start(out=old_sb[:], in_=old)

        neg_scores = sb.tile([P, I], F32, name="neg_scores", tag="val_pool", align_bytes=64)
        neg_max = sb.tile([P, 1], F32, name="neg_max")
        nc.vector.tensor_scalar(neg_scores[:], scores[:], -1.0, None, ALU.mult, ALU.min, accum_out=neg_max[:])
        p = sb.tile([P, I], F32, name="p", tag="gout_raw")
        z = sb.tile([P, 1], F32, name="z")
        nc.scalar.activation(p[:], neg_scores[:], ACT.Exp, bias=neg_max[:], scale=-1.0, accum_out=z[:])

        u = sb.tile([P, I], F32, name="u")
        nc.vector.scalar_tensor_tensor(u[:], neg_scores[:], bonus_col[:], c0[:], ALU.mult, ALU.add)
        pu = sb.tile([P, I], F32, name="pu")
        s = sb.tile([P, 1], F32, name="s")
        nc.vector.scalar_tensor_tensor(pu[:], p[:], 1.0, u[:], ALU.mult, ALU.mult, accum_out=s[:])
        inv_z = sb.tile([P, 1], F32, name="inv_z", tag="bonus_col")
        nc.vector.reciprocal(inv_z[:], z[:])
        w = sb.tile([P, I], F32, name="w")
        nc.vector.tensor_scalar(w[:], u[:], z[:], s[:], ALU.mult, ALU.subtract)
        row_factor = sb.tile([P, 1], F32, name="row_factor")
        nc.vector.scalar_tensor_tensor(row_factor[:], inv_z[:], 512.0, inv_z[:], ALU.mult, ALU.mult)
        nc.vector.tensor_tensor(placed[:].indirect(offsets[:]), p[:], w[:], ALU.mult)

        first = 0
        for n, width in enumerate(STORE_WIDTHS):
            cols = slice(first, first + width)
            result = sb.tile([P, width], F32, name="result_%d" % n)
            nc.vector.scalar_tensor_tensor(result[:], placed[:, cols], row_factor[:], old_sb[:, cols], ALU.mult, ALU.add)
            queue = nc.sync if n % 2 == 0 else nc.scalar
            queue.dma_start(out=out[:, cols], in_=result[:])
            first = first + width
